import numpy as np
import ml_dtypes


def mxq(x, axis, fmt="e4m3"):
    dtype, down = {"e4m3": (ml_dtypes.float8_e4m3fn, 7), "e5m2": (ml_dtypes.float8_e5m2, 14)}[fmt]
    v = np.moveaxis(np.asarray(x, np.float32).astype(ml_dtypes.bfloat16).astype(np.float64), axis, -1)
    blocks = v.reshape(v.shape[:-1] + (-1, 32))
    amax = np.abs(blocks).max(-1, keepdims=True)
    byte = np.maximum(np.where(amax > 0, np.frexp(amax)[1] - 1 + 127, 0) - down, 1)
    scale = np.exp2(byte - 127.0)
    codes = (blocks / scale).astype(np.float32).astype(dtype).astype(np.float64)
    return np.moveaxis((codes * scale).reshape(v.shape), -1, axis)


WIDE = False


def mx_kscale(k):
    if not WIDE:
        return np.ones(k)
    levels = np.array([10, -10, 5, -5, 0])
    if k % 512:
        return np.exp2(np.random.permutation(np.resize(levels, k // 32))).repeat(32)
    a = np.empty((k // 512, 16))
    for p in range(k // 512):
        a[p, :8] = np.random.permutation(np.resize(levels, 8))
        for g in range(8):
            far = levels[np.abs(levels - a[p, g]) >= 10]
            a[p, g + 8] = far[np.random.randint(len(far))]
    return np.exp2(a.ravel()).repeat(32)


def f64(x):
    return np.asarray(x).astype(np.float64)


def striped(idx):
    return np.tile(idx.reshape(-1, 16).T, (8, 1)).astype(np.uint16)


def unstriped(offs):
    return offs[:16].T.reshape(-1).astype(np.int64)


def striped8(idx):
    return np.concatenate([x.reshape(-1, 16).T for x in idx]).astype(np.uint16)


def runs(offs, k):
    lists = np.stack([offs[16 * r : 16 * r + 16].T.reshape(-1) for r in range(8)]).astype(np.int64)
    return lists[np.arange(k) % 512 // 64]


def pack_weight(w):
    k, n = w.shape
    w = f64(np.asarray(w, np.float32).astype(ml_dtypes.bfloat16)).reshape(k // 32, 32, n)
    amax = np.abs(w).max(1)
    byte = np.clip(np.where(amax > 0, np.frexp(amax)[1] - 1 + 127 - 7, 1), 1, 254)
    scaled = (w * np.exp2(127.0 - byte)[:, None, :]).reshape(k, n).astype(np.float32)
    words = np.ascontiguousarray(scaled.reshape(k // 512, 128, 4, n).transpose(0, 1, 3, 2)).astype(ml_dtypes.float8_e4m3fn).view(np.uint8)
    return words, np.ascontiguousarray(byte.astype(np.uint8).reshape(k // 512, 16, n))


def unpack_weight(words, scales):
    g, p, n, _ = words.shape
    vals = np.ascontiguousarray(words).view(ml_dtypes.float8_e4m3fn).astype(np.float64) * np.repeat(np.exp2(scales.astype(np.float64) - 127.0), 8, axis=1)[..., None]
    return vals.transpose(0, 1, 3, 2).reshape(g * 512, n)


def sigmoid(v):
    return 1.0 / (1.0 + np.exp(-np.maximum(v, -700.0)))


K, T, S, N, G, H = 512, 2048, 512, 512, 2048, 512


def setup_inputs():
    n = np.random.standard_normal
    s = mx_kscale(K)[:, None]
    u = mx_kscale(H)
    packed_xT = pack_weight(n((K, T)) * s)
    packed_dT = pack_weight(n((K, G)) / s)
    return {
        "x_words": packed_xT[0],
        "x_scales": packed_xT[1],
        "d_words": packed_dT[0],
        "d_scales": packed_dT[1],
        "gn": (np.random.uniform(0.5, 1.5, (H, 1)) * u[:, None]).astype(np.float32),
        "w1": (n((H, N)) / np.sqrt(H) / u[:, None]).astype(np.float32),
        "offs": striped(np.random.permutation(T)[:S]),
        "kidx": striped8(np.random.randint(0, G, (8, H))),
        "n1": striped8(np.stack([np.random.permutation(S) for _ in range(8)])),
        "n2": striped8(np.stack([np.random.permutation(S) for _ in range(8)])),
    }


def reference(x_words, x_scales, d_words, d_scales, gn, w1, offs, kidx, n1, n2):
    d_kidx = unpack_weight(d_words, d_scales)[np.arange(K)[:, None], runs(kidx, K)]
    xq = unpack_weight(x_words, x_scales)[:, unstriped(offs)]
    s = 0.0625 * (d_kidx.T @ xq)
    sg = sigmoid(s[np.arange(H)[:, None], runs(n1, H)] - (s[np.arange(H)[:, None], runs(n2, H)]))
    z = f64(gn) * (s * sg)
    return mxq(f64(w1), 0, "e4m3").T @ mxq(z, 0, "e4m3")

@@ -1,0 +1,186 @@
+from contextlib import ExitStack
+
+import concourse.mybir as mybir
+
+K, T, S, N, G, H = 512, 2048, 512, 512, 2048, 512
+FLOPS = 2 * K * H * S + 2 * H * N * S
+
+F32 = mybir.dt.float32
+BF16 = mybir.dt.bfloat16
+I32 = mybir.dt.int32
+U32 = mybir.dt.uint32
+U16 = mybir.dt.uint16
+U8 = mybir.dt.uint8
+FP8X4 = mybir.dt.float8_e4m3fn_x4
+ACT = mybir.ActivationFunctionType
+ALU = mybir.AluOpType
+
+P = 128
+PACK = 4
+HALF = S // 2
+CHUNK = 128
+
+
+def tile_picked_scorecmp_none_p_kernel(tc, x_words, x_scales, d_words, d_scales, gn, w1, offs, kidx, n1, n2, out):
+    nc = tc.nc
+    with ExitStack() as ctx:
+        sb = ctx.enter_context(tc.tile_pool(name="sb", bufs=1))
+        ps = ctx.enter_context(tc.psum_pool(name="ps", bufs=1))
+
+        def tile(shape, dtype, name, tag=None):
+            return sb.tile(shape, dtype, name=name, tag=tag or name, align_bytes=64)
+
+        kidx_sb = tile([P, H // 16], U16, "kidx_sb")
+        offs_sb = tile([P, S // 16], U16, "offs_sb")
+        n1_sb = tile([P, S // 16], U16, "n1_sb")
+        n2_sb = tile([P, S // 16], U16, "n2_sb")
+        d_byte_table = tile([P, G], U8, "d_byte_table")
+        x_byte_table = tile([P, T], U8, "x_byte_table", "slot_a")
+        d_word_table = tile([P, G], U32, "d_word_table", "slot_b")
+        x_word_table = tile([P, T], U32, "x_word_table")
+        gn_sb = tile([P, PACK], F32, "gn_sb")
+
+        nc.vector.memset(d_byte_table[:].bitcast(I32), 0)
+        nc.vector.memset(x_byte_table[:].bitcast(I32), 0)
+        nc.sync.dma_start(kidx_sb[:], kidx)
+        nc.sync.dma_start(offs_sb[:], offs)
+        nc.sync.dma_start(n1_sb[:], n1)
+        nc.sync.dma_start(n2_sb[:], n2)
+        d_rows = d_scales[0].rearrange("(r e) c -> e r c", e=2)
+        for e in range(2):
+            nc.sync.dma_start(d_byte_table[e:P:16, :].bitcast(I32), d_rows[e].bitcast(I32))
+        nc.sync.dma_start(d_word_table[:].bitcast(I32), d_words[0].rearrange("p c r -> p (c r)").bitcast(I32))
+        nc.sync.dma_start(x_word_table[:].bitcast(I32), x_words[0].rearrange("p c r -> p (c r)").bitcast(I32))
+        for q in range(4):
+            nc.scalar.dma_start(x_byte_table[32 * q : 32 * q + 4, :].bitcast(I32), x_scales[0, 4 * q : 4 * q + 4, :].bitcast(I32))
+        nc.gpsimd.dma_start(gn_sb[:], gn.rearrange("(p t) o -> p (t o)", t=PACK))
+
+        d_bytes_picked = tile([P, H], U8, "d_bytes_picked", "slot_c")
+        nc.vector.tensor_copy(d_bytes_picked[:], d_byte_table[:].indirect(kidx_sb[:]))
+        key_scales = tile([P, H], U8, "key_scales")
+        nc.vector.tensor_copy(
+            key_scales[:].rearrange("p (t c i) -> p c t i", t=PACK, i=16),
+            d_bytes_picked[:].rearrange("p (c i t) -> p c t i", t=PACK, i=16),
+        )
+        for e in range(2):
+            nc.scalar.dma_start(key_scales[2 + e : P : 32, :].bitcast(I32), key_scales[16 + e : P : 32, :].bitcast(I32))
+
+        d_words_picked = tile([P, H], U32, "d_words_picked", "slot_c")
+        nc.vector.tensor_copy(d_words_picked[:], d_word_table[:].indirect(kidx_sb[:]))
+        key_words = tile([P, H], U32, "key_words")
+        nc.vector.tensor_copy(
+            key_words[:].rearrange("p (t c i) -> p c t i", t=PACK, i=4),
+            d_words_picked[:].rearrange("p (c i t) -> p c t i", t=PACK, i=4),
+        )
+        query_scales = tile([P, S], U8, "query_scales", "slot_b")
+        nc.vector.tensor_copy(query_scales[:], x_byte_table[:].indirect(offs_sb[:]))
+        w_rows = w1.rearrange("(p t) n -> p t n", t=PACK)
+        w_raw = []
+        for u in range(2):
+            w_raw.append(tile([P, PACK, N // 2], F32, "w_raw%d" % u, ("slot_a", "slot_c")[u]))
+            nc.sync.dma_start(w_raw[u][:], w_rows[:, :, u * N // 2 : (u + 1) * N // 2])
+        query_words = [tile([P, HALF], U32, "query_words%d" % h) for h in range(2)]
+        for h in range(2):
+            nc.vector.tensor_copy(query_words[h][:], x_word_table[:].indirect(offs_sb[:, h * HALF // 16 : (h + 1) * HALF // 16]))
+
+        s_bank = [[ps.tile([P, 2, HALF], F32, name="s_bank%d%d" % (h, u), tag="s_bank%d%d" % (h, u)) for u in range(2)] for h in range(2)]
+        s = [tile([P, S], F32, "s%d" % t) for t in range(PACK)]
+        for u in range(2):
+            for h in range(2):
+                cols = slice(h * HALF, (h + 1) * HALF)
+                for e in range(2):
+                    t = 2 * u + e
+                    nc.tensor.matmul_mx(
+                        out=s_bank[h][u][:, e, :],
+                        lhsT=key_words[:, t * P : (t + 1) * P].bitcast(FP8X4),
+                        lhsT_scale=key_scales[:, t * P : (t + 1) * P],
+                        rhs=query_words[h][:].bitcast(FP8X4),
+                        rhs_scale=query_scales[:, cols],
+                        start=True,
+                        stop=True,
+                    )
+                for e in range(2):
+                    t = 2 * u + e
+                    if h == 0:
+                        nc.scalar.activation(s[t][:, cols], s_bank[h][u][:, e, :], ACT.Copy, scale=0.0625)
+                    else:
+                        nc.vector.tensor_scalar(s[t][:, cols], s_bank[h][u][:, e, :], 0.0625, None, ALU.mult)
+
+        w_words = tile([P, N], U32, "w_words")
+        w_scales = tile([P, N], U8, "w_scales")
+
+        def quantize_w():
+            for u in range(2):
+                cols = slice(u * N // 2, (u + 1) * N // 2)
+                w_woven = tile([P, N // 2 * PACK], BF16, "w_woven%d" % u)
+                dst = w_woven[:].rearrange("p (c i t) -> p c t i", t=PACK, i=4)
+                src = w_raw[u][:].rearrange("p t (c i) -> p c t i", i=4)
+                if u == 0:
+                    nc.scalar.copy(dst, src)
+                else:
+                    nc.vector.tensor_copy(dst, src)
+                nc.vector.quantize_mx(out=w_words[:, cols].bitcast(FP8X4), scales=w_scales[:, cols], in_=w_woven[:])
+
+        out_rows = out.rearrange("(u p) j -> p u j", p=P)
+
+        def compare(c):
+            entries = slice(c * CHUNK // 16, (c + 1) * CHUNK // 16)
+            second = tile([P, PACK, CHUNK], F32, "second%d" % c, "slot_a" if c == 2 else None)
+            diff = tile([P, PACK, CHUNK], F32, "diff%d" % c)
+            for t in range(PACK):
+                nc.scalar.activation(second[:, t, :], s[t][:].indirect(n2_sb[:, entries]), ACT.Copy)
+                nc.vector.tensor_tensor(diff[:, t, :], s[t][:].indirect(n1_sb[:, entries]), second[:, t, :], ALU.subtract)
+            sg = tile([P, PACK, CHUNK], F32, "sg%d" % c)
+            if c == S // CHUNK - 1:
+                for t in range(PACK):
+                    nc.scalar.activation(sg[:, t, :], diff[:, t, :], ACT.Sigmoid)
+            else:
+                nc.scalar.activation(sg[:], diff[:], ACT.Sigmoid)
+            return sg
+
+        def finish(c, sg):
+            cols = slice(c * CHUNK, (c + 1) * CHUNK)
+            z = tile([P, PACK, CHUNK], BF16, "z%d" % c)
+            for t in range(PACK):
+                nc.vector.scalar_tensor_tensor(z[:, t, :], s[t][:, cols], gn_sb[:, t : t + 1], sg[:, t, :], ALU.mult, ALU.mult)
+            z_woven = tile([P, CHUNK * PACK], BF16, "z_woven%d" % c)
+            nc.vector.tensor_copy(
+                z_woven[:].rearrange("p (c i t) -> p c t i", t=PACK, i=4),
+                z[:].rearrange("p t (c i) -> p c t i", i=4),
+            )
+            z_words = tile([P, CHUNK], U32, "z_words%d" % c)
+            z_scales = tile([P, CHUNK], U8, "z_scales%d" % c)
+            nc.vector.quantize_mx(out=z_words[:].bitcast(FP8X4), scales=z_scales[:], in_=z_woven[:])
+            parts = 2 if c == S // CHUNK - 1 else 1
+            width = N // P // parts
+            for part in range(parts):
+                name = "out_bank%d_%d" % (c, part)
+                bank = ps.tile([P, width, CHUNK], F32, name=name, tag="s_bank00" if part == 1 else name)
+                for e in range(width):
+                    u = part * width + e
+                    nc.tensor.matmul_mx(
+                        out=bank[:, e, :],
+                        lhsT=w_words[:, u * P : (u + 1) * P].bitcast(FP8X4),
+                        lhsT_scale=w_scales[:, u * P : (u + 1) * P],
+                        rhs=z_words[:].bitcast(FP8X4),
+                        rhs_scale=z_scales[:],
+                        start=True,
+                        stop=True,
+                    )
+                result = tile([P, width, CHUNK], F32, "result%d_%d" % (c, part))
+                rows = out_rows[:, part * width : (part + 1) * width, cols]
+                if part == 0:
+                    nc.scalar.copy(result[:], bank[:])
+                    (nc.scalar if parts == 2 else nc.sync).dma_start(rows, result[:])
+                else:
+                    nc.vector.tensor_copy(result[:], bank[:])
+                    nc.sync.dma_start(rows, result[:])
+
+        chunks = S // CHUNK
+        gates = [compare(0), compare(1)]
+        quantize_w()
+        finish(0, gates[0])
+        for c in range(2, chunks):
+            gates.append(compare(c))
+            finish(c - 1, gates[c - 1])
+        finish(chunks - 1, gates[chunks - 1])

@@ -55,6 +55,9 @@ def tile_picked_scorecmp_none_p_kernel(tc, x_words, x_scales, d_words, d_scales,
             nc.scalar.dma_start(x_byte_table[32 * q : 32 * q + 4, :].bitcast(I32), x_scales[0, 4 * q : 4 * q + 4, :].bitcast(I32))
         nc.gpsimd.dma_start(gn_sb[:], gn.rearrange("(p t) o -> p (t o)", t=PACK))
 
+        warm = tile([P, 1], F32, "warm")
+        nc.scalar.activation(warm[:], gn_sb[:, 0:1], ACT.Sigmoid)
+
         d_bytes_picked = tile([P, H], U8, "d_bytes_picked", "slot_c")
         nc.vector.tensor_copy(d_bytes_picked[:], d_byte_table[:].indirect(kidx_sb[:]))
         key_scales = tile([P, H], U8, "key_scales")

@@ -30,29 +30,31 @@ def tile_picked_scorecmp_none_p_kernel(tc, x_words, x_scales, d_words, d_scales,
         def tile(shape, dtype, name, tag=None):
             return sb.tile(shape, dtype, name=name, tag=tag or name, align_bytes=64)
 
+        def entries(h):
+            return slice(h * HALF // 16, (h + 1) * HALF // 16)
+
         kidx_sb = tile([P, H // 16], U16, "kidx_sb")
         offs_sb = tile([P, S // 16], U16, "offs_sb")
         n1_sb = tile([P, S // 16], U16, "n1_sb")
         n2_sb = tile([P, S // 16], U16, "n2_sb")
-        d_byte_table = tile([P, G], U8, "d_byte_table")
-        x_byte_table = tile([P, T], U8, "x_byte_table", "slot_a")
-        d_word_table = tile([P, G], U32, "d_word_table", "slot_b")
+        d_byte_table = tile([P, G], U8, "d_byte_table", "slot_a")
+        x_byte_table = tile([P, T], U8, "x_byte_table", "slot_e")
+        d_word_table = tile([P, G], U32, "d_word_table")
         x_word_table = tile([P, T], U32, "x_word_table")
         gn_sb = tile([P, PACK], F32, "gn_sb")
+        w_rows = w1.rearrange("(p t) n -> p t n", t=PACK)
 
         nc.vector.memset(d_byte_table[:].bitcast(I32), 0)
-        nc.vector.memset(x_byte_table[:].bitcast(I32), 0)
+        nc.gpsimd.memset(x_byte_table[:].bitcast(I32), 0)
         nc.sync.dma_start(kidx_sb[:], kidx)
         nc.sync.dma_start(offs_sb[:], offs)
-        nc.sync.dma_start(n1_sb[:], n1)
-        nc.sync.dma_start(n2_sb[:], n2)
-        d_rows = d_scales[0].rearrange("(r e) c -> e r c", e=2)
-        for e in range(2):
-            nc.sync.dma_start(d_byte_table[e:P:16, :].bitcast(I32), d_rows[e].bitcast(I32))
+        nc.sync.dma_start(d_byte_table[0:P:8, :].bitcast(I32), d_scales[0].bitcast(I32))
+        for q, queue in enumerate((nc.scalar, nc.scalar, nc.sync, nc.sync)):
+            queue.dma_start(x_byte_table[32 * q : 32 * q + 4, :].bitcast(I32), x_scales[0, 4 * q : 4 * q + 4, :].bitcast(I32))
         nc.sync.dma_start(d_word_table[:].bitcast(I32), d_words[0].rearrange("p c r -> p (c r)").bitcast(I32))
         nc.sync.dma_start(x_word_table[:].bitcast(I32), x_words[0].rearrange("p c r -> p (c r)").bitcast(I32))
-        for q in range(4):
-            nc.scalar.dma_start(x_byte_table[32 * q : 32 * q + 4, :].bitcast(I32), x_scales[0, 4 * q : 4 * q + 4, :].bitcast(I32))
+        nc.sync.dma_start(n1_sb[:], n1)
+        nc.sync.dma_start(n2_sb[:], n2)
         nc.gpsimd.dma_start(gn_sb[:], gn.rearrange("(p t) o -> p (t o)", t=PACK))
 
         warm = tile([P, 1], F32, "warm")
@@ -65,102 +67,97 @@ def tile_picked_scorecmp_none_p_kernel(tc, x_words, x_scales, d_words, d_scales,
             key_scales[:].rearrange("p (t c i) -> p c t i", t=PACK, i=16),
             d_bytes_picked[:].rearrange("p (c i t) -> p c t i", t=PACK, i=16),
         )
-        for e in range(2):
-            nc.scalar.dma_start(key_scales[2 + e : P : 32, :].bitcast(I32), key_scales[16 + e : P : 32, :].bitcast(I32))
+        for r in range(1, 4):
+            nc.sync.dma_start(key_scales[r:P:32, :].bitcast(I32), key_scales[8 * r : P : 32, :].bitcast(I32))
 
-        d_words_picked = tile([P, H], U32, "d_words_picked", "slot_c")
+        query_scales = tile([P, S], U8, "query_scales", "slot_c")
+        nc.vector.tensor_copy(query_scales[:], x_byte_table[:].indirect(offs_sb[:]))
+        w_raw = tile([P, PACK, N], F32, "w_raw", "slot_e")
+        nc.sync.dma_start(w_raw[:], w_rows)
+
+        d_words_picked = tile([P, H], U32, "d_words_picked", "slot_a")
         nc.vector.tensor_copy(d_words_picked[:], d_word_table[:].indirect(kidx_sb[:]))
         key_words = tile([P, H], U32, "key_words")
         nc.vector.tensor_copy(
             key_words[:].rearrange("p (t c i) -> p c t i", t=PACK, i=4),
             d_words_picked[:].rearrange("p (c i t) -> p c t i", t=PACK, i=4),
         )
-        query_scales = tile([P, S], U8, "query_scales", "slot_b")
-        nc.vector.tensor_copy(query_scales[:], x_byte_table[:].indirect(offs_sb[:]))
-        w_rows = w1.rearrange("(p t) n -> p t n", t=PACK)
-        w_raw = []
-        for u in range(2):
-            w_raw.append(tile([P, PACK, N // 2], F32, "w_raw%d" % u, ("slot_a", "slot_c")[u]))
-            nc.sync.dma_start(w_raw[u][:], w_rows[:, :, u * N // 2 : (u + 1) * N // 2])
         query_words = [tile([P, HALF], U32, "query_words%d" % h) for h in range(2)]
         for h in range(2):
-            nc.vector.tensor_copy(query_words[h][:], x_word_table[:].indirect(offs_sb[:, h * HALF // 16 : (h + 1) * HALF // 16]))
-
-        s_bank = [[ps.tile([P, 2, HALF], F32, name="s_bank%d%d" % (h, u), tag="s_bank%d%d" % (h, u)) for u in range(2)] for h in range(2)]
-        s = [tile([P, S], F32, "s%d" % t) for t in range(PACK)]
-        for u in range(2):
-            for h in range(2):
-                cols = slice(h * HALF, (h + 1) * HALF)
-                for e in range(2):
-                    t = 2 * u + e
-                    nc.tensor.matmul_mx(
-                        out=s_bank[h][u][:, e, :],
-                        lhsT=key_words[:, t * P : (t + 1) * P].bitcast(FP8X4),
-                        lhsT_scale=key_scales[:, t * P : (t + 1) * P],
-                        rhs=query_words[h][:].bitcast(FP8X4),
-                        rhs_scale=query_scales[:, cols],
-                        start=True,
-                        stop=True,
-                    )
-                for e in range(2):
-                    t = 2 * u + e
-                    if h == 0:
-                        nc.scalar.activation(s[t][:, cols], s_bank[h][u][:, e, :], ACT.Copy, scale=0.0625)
-                    else:
-                        nc.vector.tensor_scalar(s[t][:, cols], s_bank[h][u][:, e, :], 0.0625, None, ALU.mult)
+            nc.vector.tensor_copy(query_words[h][:], x_word_table[:].indirect(offs_sb[:, entries(h)]))
 
         w_words = tile([P, N], U32, "w_words")
         w_scales = tile([P, N], U8, "w_scales")
 
-        def quantize_w():
-            for u in range(2):
-                cols = slice(u * N // 2, (u + 1) * N // 2)
-                w_woven = tile([P, N // 2 * PACK], BF16, "w_woven%d" % u)
-                dst = w_woven[:].rearrange("p (c i t) -> p c t i", t=PACK, i=4)
-                src = w_raw[u][:].rearrange("p t (c i) -> p c t i", i=4)
-                if u == 0:
-                    nc.scalar.copy(dst, src)
+        s = [tile([P, S], F32, "s%d" % t) for t in range(PACK)]
+        for t in range(PACK):
+            for h in range(2):
+                cols = slice(h * HALF, (h + 1) * HALF)
+                s_bank = ps.tile([P, HALF], F32, name="s_bank%d%d" % (t, h), tag="bank%d" % (2 * t + h))
+                nc.tensor.matmul_mx(
+                    out=s_bank[:],
+                    lhsT=key_words[:, t * P : (t + 1) * P].bitcast(FP8X4),
+                    lhsT_scale=key_scales[:, t * P : (t + 1) * P],
+                    rhs=query_words[h][:].bitcast(FP8X4),
+                    rhs_scale=query_scales[:, cols],
+                    start=True,
+                    stop=True,
+                )
+                if h == 0:
+                    nc.scalar.activation(s[t][:, cols], s_bank[:], ACT.Copy, scale=0.0625)
                 else:
-                    nc.vector.tensor_copy(dst, src)
-                nc.vector.quantize_mx(out=w_words[:, cols].bitcast(FP8X4), scales=w_scales[:, cols], in_=w_woven[:])
+                    nc.vector.tensor_scalar(s[t][:, cols], s_bank[:], 0.0625, None, ALU.mult)
+
+        w_woven = [tile([P, N // 2 * PACK], BF16, "w_woven0"), tile([P, N // 2 * PACK], BF16, "w_woven1")]
+        for u in range(2):
+            dst = w_woven[u][:].rearrange("p (c i t) -> p c t i", t=PACK, i=4)
+            src = w_raw[:, :, u * N // 2 : (u + 1) * N // 2].rearrange("p t (c i) -> p c t i", i=4)
+            if u == 0:
+                nc.scalar.copy(dst, src)
+            else:
+                nc.vector.tensor_copy(dst, src)
+        for u in (1, 0):
+            cols = slice(u * N // 2, (u + 1) * N // 2)
+            nc.vector.quantize_mx(out=w_words[:, cols].bitcast(FP8X4), scales=w_scales[:, cols], in_=w_woven[u][:])
 
         out_rows = out.rearrange("(u p) j -> p u j", p=P)
+        chunks = S // CHUNK
 
         def compare(c):
-            entries = slice(c * CHUNK // 16, (c + 1) * CHUNK // 16)
-            second = tile([P, PACK, CHUNK], F32, "second%d" % c, "slot_a" if c == 2 else None)
+            part = slice(c * CHUNK // 16, (c + 1) * CHUNK // 16)
+            second = tile([P, PACK, CHUNK], F32, "second%d" % c)
             diff = tile([P, PACK, CHUNK], F32, "diff%d" % c)
             for t in range(PACK):
-                nc.scalar.activation(second[:, t, :], s[t][:].indirect(n2_sb[:, entries]), ACT.Copy)
-                nc.vector.tensor_tensor(diff[:, t, :], s[t][:].indirect(n1_sb[:, entries]), second[:, t, :], ALU.subtract)
+                nc.scalar.activation(second[:, t, :], s[t][:].indirect(n2_sb[:, part]), ACT.Copy)
+                nc.vector.tensor_tensor(diff[:, t, :], s[t][:].indirect(n1_sb[:, part]), second[:, t, :], ALU.subtract)
             sg = tile([P, PACK, CHUNK], F32, "sg%d" % c)
-            if c == S // CHUNK - 1:
+            if c == chunks - 1:
                 for t in range(PACK):
                     nc.scalar.activation(sg[:, t, :], diff[:, t, :], ACT.Sigmoid)
             else:
                 nc.scalar.activation(sg[:], diff[:], ACT.Sigmoid)
             return sg
 
-        def finish(c, sg):
+        def finish(c, sg, banks, readers):
+            name = "%d" % c
+            width = CHUNK
             cols = slice(c * CHUNK, (c + 1) * CHUNK)
-            z = tile([P, PACK, CHUNK], BF16, "z%d" % c)
+            z = tile([P, PACK, CHUNK], BF16, "z" + name)
             for t in range(PACK):
                 nc.vector.scalar_tensor_tensor(z[:, t, :], s[t][:, cols], gn_sb[:, t : t + 1], sg[:, t, :], ALU.mult, ALU.mult)
-            z_woven = tile([P, CHUNK * PACK], BF16, "z_woven%d" % c)
-            nc.vector.tensor_copy(
+            z_woven = tile([P, width * PACK], BF16, "z_woven" + name)
+            (nc.scalar.copy if c in () else nc.vector.tensor_copy)(
                 z_woven[:].rearrange("p (c i t) -> p c t i", t=PACK, i=4),
                 z[:].rearrange("p t (c i) -> p c t i", i=4),
             )
-            z_words = tile([P, CHUNK], U32, "z_words%d" % c)
-            z_scales = tile([P, CHUNK], U8, "z_scales%d" % c)
+            z_words = tile([P, width], U32, "z_words" + name)
+            z_scales = tile([P, width], U8, "z_scales" + name)
             nc.vector.quantize_mx(out=z_words[:].bitcast(FP8X4), scales=z_scales[:], in_=z_woven[:])
-            parts = 2 if c == S // CHUNK - 1 else 1
-            width = N // P // parts
-            for part in range(parts):
-                name = "out_bank%d_%d" % (c, part)
-                bank = ps.tile([P, width, CHUNK], F32, name=name, tag="s_bank00" if part == 1 else name)
-                for e in range(width):
-                    u = part * width + e
+            blocks = N // P // len(banks)
+            for part, tag in enumerate(banks):
+                bank = ps.tile([P, blocks, width], F32, name="out_bank%s_%d" % (name, part), tag=tag)
+                for e in range(blocks):
+                    u = part * blocks + e
                     nc.tensor.matmul_mx(
                         out=bank[:, e, :],
                         lhsT=w_words[:, u * P : (u + 1) * P].bitcast(FP8X4),
@@ -170,20 +167,16 @@ def tile_picked_scorecmp_none_p_kernel(tc, x_words, x_scales, d_words, d_scales,
                         start=True,
                         stop=True,
                     )
-                result = tile([P, width, CHUNK], F32, "result%d_%d" % (c, part))
-                rows = out_rows[:, part * width : (part + 1) * width, cols]
-                if part == 0:
-                    nc.scalar.copy(result[:], bank[:])
-                    (nc.scalar if parts == 2 else nc.sync).dma_start(rows, result[:])
-                else:
+                result = tile([P, blocks, width], F32, "result%s_%d" % (name, part))
+                rows = out_rows[:, part * blocks : (part + 1) * blocks, cols]
+                if readers[part] == "vector":
                     nc.vector.tensor_copy(result[:], bank[:])
-                    nc.sync.dma_start(rows, result[:])
+                else:
+                    nc.scalar.copy(result[:], bank[:])
+                (nc.scalar if readers[part] == "scalar_own" else nc.sync).dma_start(rows, result[:])
 
-        chunks = S // CHUNK
-        gates = [compare(0), compare(1)]
-        quantize_w()
-        finish(0, gates[0])
-        for c in range(2, chunks):
+        gates = [compare(0)]
+        for c in range(1, chunks):
             gates.append(compare(c))
-            finish(c - 1, gates[c - 1])
-        finish(chunks - 1, gates[chunks - 1])
+            finish(c - 1, gates[c - 1], ("bank%d" % (c - 1),), ("scalar",))
+        finish(chunks - 1, gates[chunks - 1], ("bank3", "bank4"), ("scalar_own", "vector"))

@@ -39,8 +39,8 @@ def tile_picked_scorecmp_none_p_kernel(tc, x_words, x_scales, d_words, d_scales,
         n2_sb = tile([P, S // 16], U16, "n2_sb")
         d_byte_table = tile([P, G], U8, "d_byte_table", "slot_a")
         x_byte_table = tile([P, T], U8, "x_byte_table", "slot_e")
-        d_word_table = tile([P, G], U32, "d_word_table")
-        x_word_table = tile([P, T], U32, "x_word_table")
+        d_word_table = tile([P, G], U32, "d_word_table", "slot_b")
+        x_word_table = tile([P, T], U32, "x_word_table", "slot_d")
         gn_sb = tile([P, PACK], F32, "gn_sb")
         w_rows = w1.rearrange("(p t) n -> p t n", t=PACK)
 
@@ -72,11 +72,13 @@ def tile_picked_scorecmp_none_p_kernel(tc, x_words, x_scales, d_words, d_scales,
 
         query_scales = tile([P, S], U8, "query_scales", "slot_c")
         nc.vector.tensor_copy(query_scales[:], x_byte_table[:].indirect(offs_sb[:]))
-        w_raw = tile([P, PACK, N], F32, "w_raw", "slot_e")
-        nc.sync.dma_start(w_raw[:], w_rows)
+        w_raw = [tile([P, PACK, N // 2], F32, "w_raw0", "slot_e")]
+        nc.sync.dma_start(w_raw[0][:], w_rows[:, :, : N // 2])
 
         d_words_picked = tile([P, H], U32, "d_words_picked", "slot_a")
         nc.vector.tensor_copy(d_words_picked[:], d_word_table[:].indirect(kidx_sb[:]))
+        w_raw.append(tile([P, PACK, N // 2], F32, "w_raw1", "slot_b"))
+        nc.sync.dma_start(w_raw[1][:], w_rows[:, :, N // 2 :])
         key_words = tile([P, H], U32, "key_words")
         nc.vector.tensor_copy(
             key_words[:].rearrange("p (t c i) -> p c t i", t=PACK, i=4),
@@ -108,12 +110,12 @@ def tile_picked_scorecmp_none_p_kernel(tc, x_words, x_scales, d_words, d_scales,
                 else:
                     nc.vector.tensor_scalar(s[t][:, cols], s_bank[:], 0.0625, None, ALU.mult)
 
-        w_woven = [tile([P, N // 2 * PACK], BF16, "w_woven0"), tile([P, N // 2 * PACK], BF16, "w_woven1")]
+        w_woven = [tile([P, N // 2 * PACK], BF16, "w_woven0", "slot_d"), tile([P, N // 2 * PACK], BF16, "w_woven1")]
         for u in range(2):
             dst = w_woven[u][:].rearrange("p (c i t) -> p c t i", t=PACK, i=4)
-            src = w_raw[:, :, u * N // 2 : (u + 1) * N // 2].rearrange("p t (c i) -> p c t i", i=4)
+            src = w_raw[u][:].rearrange("p t (c i) -> p c t i", i=4)
             if u == 0:
-                nc.scalar.copy(dst, src)
+                nc.gpsimd.tensor_scalar(dst, src, 1.0, 0.0, ALU.mult, ALU.add)
             else:
                 nc.vector.tensor_copy(dst, src)
         for u in (1, 0):
@@ -146,7 +148,7 @@ def tile_picked_scorecmp_none_p_kernel(tc, x_words, x_scales, d_words, d_scales,
             for t in range(PACK):
                 nc.vector.scalar_tensor_tensor(z[:, t, :], s[t][:, cols], gn_sb[:, t : t + 1], sg[:, t, :], ALU.mult, ALU.mult)
             z_woven = tile([P, width * PACK], BF16, "z_woven" + name)
-            (nc.scalar.copy if c in () else nc.vector.tensor_copy)(
+            (nc.scalar.copy if c in (1, 2) else nc.vector.tensor_copy)(
                 z_woven[:].rearrange("p (c i t) -> p c t i", t=PACK, i=4),
                 z[:].rearrange("p t (c i) -> p c t i", i=4),
             )

from contextlib import ExitStack

import concourse.mybir as mybir

K, T, S, N, G, H = 512, 2048, 512, 512, 2048, 512
FLOPS = 2 * K * H * S + 2 * H * N * S

F32 = mybir.dt.float32
BF16 = mybir.dt.bfloat16
I32 = mybir.dt.int32
U32 = mybir.dt.uint32
U16 = mybir.dt.uint16
U8 = mybir.dt.uint8
FP8X4 = mybir.dt.float8_e4m3fn_x4
ACT = mybir.ActivationFunctionType
ALU = mybir.AluOpType

P = 128
PACK = 4
HALF = S // 2
CHUNK = 128


def tile_picked_scorecmp_none_p_kernel(tc, x_words, x_scales, d_words, d_scales, gn, w1, offs, kidx, n1, n2, out):
    nc = tc.nc
    with ExitStack() as ctx:
        sb = ctx.enter_context(tc.tile_pool(name="sb", bufs=1))
        ps = ctx.enter_context(tc.psum_pool(name="ps", bufs=1))

        def tile(shape, dtype, name, tag=None):
            return sb.tile(shape, dtype, name=name, tag=tag or name, align_bytes=64)

        def entries(h):
            return slice(h * HALF // 16, (h + 1) * HALF // 16)

        kidx_sb = tile([P, H // 16], U16, "kidx_sb")
        offs_sb = tile([P, S // 16], U16, "offs_sb")
        n1_sb = tile([P, S // 16], U16, "n1_sb")
        n2_sb = tile([P, S // 16], U16, "n2_sb")
        d_byte_table = tile([P, G], U8, "d_byte_table", "slot_a")
        x_byte_table = tile([P, T], U8, "x_byte_table", "slot_e")
        d_word_table = tile([P, G], U32, "d_word_table", "slot_b")
        x_word_table = tile([P, T], U32, "x_word_table", "slot_d")
        gn_sb = tile([P, PACK], F32, "gn_sb")
        w_rows = w1.rearrange("(p t) n -> p t n", t=PACK)

        nc.vector.memset(d_byte_table[:].bitcast(I32), 0)
        nc.gpsimd.memset(x_byte_table[:].bitcast(I32), 0)
        nc.sync.dma_start(kidx_sb[:], kidx)
        nc.sync.dma_start(offs_sb[:], offs)
        nc.sync.dma_start(d_byte_table[0:P:8, :].bitcast(I32), d_scales[0].bitcast(I32))
        for q, queue in enumerate((nc.scalar, nc.scalar, nc.sync, nc.sync)):
            queue.dma_start(x_byte_table[32 * q : 32 * q + 4, :].bitcast(I32), x_scales[0, 4 * q : 4 * q + 4, :].bitcast(I32))
        nc.sync.dma_start(d_word_table[:].bitcast(I32), d_words[0].rearrange("p c r -> p (c r)").bitcast(I32))
        nc.sync.dma_start(x_word_table[:].bitcast(I32), x_words[0].rearrange("p c r -> p (c r)").bitcast(I32))
        nc.sync.dma_start(n1_sb[:], n1)
        nc.sync.dma_start(n2_sb[:], n2)
        nc.gpsimd.dma_start(gn_sb[:], gn.rearrange("(p t) o -> p (t o)", t=PACK))

        warm = tile([P, 1], F32, "warm")
        nc.scalar.activation(warm[:], gn_sb[:, 0:1], ACT.Sigmoid)

        d_bytes_picked = tile([P, H], U8, "d_bytes_picked", "slot_c")
        nc.vector.tensor_copy(d_bytes_picked[:], d_byte_table[:].indirect(kidx_sb[:]))
        key_scales = tile([P, H], U8, "key_scales")
        nc.vector.tensor_copy(
            key_scales[:].rearrange("p (t c i) -> p c t i", t=PACK, i=16),
            d_bytes_picked[:].rearrange("p (c i t) -> p c t i", t=PACK, i=16),
        )
        for r in range(1, 4):
            nc.sync.dma_start(key_scales[r:P:32, :].bitcast(I32), key_scales[8 * r : P : 32, :].bitcast(I32))

        query_scales = tile([P, S], U8, "query_scales", "slot_c")
        nc.vector.tensor_copy(query_scales[:], x_byte_table[:].indirect(offs_sb[:]))
        w_raw = [tile([P, PACK, N // 2], F32, "w_raw0", "slot_e")]
        nc.sync.dma_start(w_raw[0][:], w_rows[:, :, : N // 2])

        d_words_picked = tile([P, H], U32, "d_words_picked", "slot_a")
        nc.vector.tensor_copy(d_words_picked[:], d_word_table[:].indirect(kidx_sb[:]))
        w_raw.append(tile([P, PACK, N // 2], F32, "w_raw1", "slot_b"))
        nc.sync.dma_start(w_raw[1][:], w_rows[:, :, N // 2 :])
        key_words = tile([P, H], U32, "key_words")
        nc.vector.tensor_copy(
            key_words[:].rearrange("p (t c i) -> p c t i", t=PACK, i=4),
            d_words_picked[:].rearrange("p (c i t) -> p c t i", t=PACK, i=4),
        )
        query_words = [tile([P, HALF], U32, "query_words%d" % h) for h in range(2)]
        for h in range(2):
            nc.vector.tensor_copy(query_words[h][:], x_word_table[:].indirect(offs_sb[:, entries(h)]))

        w_words = tile([P, N], U32, "w_words")
        w_scales = tile([P, N], U8, "w_scales")

        s = [tile([P, S], F32, "s%d" % t) for t in range(PACK)]
        for t in range(PACK):
            for h in range(2):
                cols = slice(h * HALF, (h + 1) * HALF)
                s_bank = ps.tile([P, HALF], F32, name="s_bank%d%d" % (t, h), tag="bank%d" % (2 * t + h))
                nc.tensor.matmul_mx(
                    out=s_bank[:],
                    lhsT=key_words[:, t * P : (t + 1) * P].bitcast(FP8X4),
                    lhsT_scale=key_scales[:, t * P : (t + 1) * P],
                    rhs=query_words[h][:].bitcast(FP8X4),
                    rhs_scale=query_scales[:, cols],
                    start=True,
                    stop=True,
                )
                if h == 0:
                    nc.scalar.activation(s[t][:, cols], s_bank[:], ACT.Copy, scale=0.0625)
                else:
                    nc.vector.tensor_scalar(s[t][:, cols], s_bank[:], 0.0625, None, ALU.mult)

        w_woven = [tile([P, N // 2 * PACK], BF16, "w_woven0", "slot_d"), tile([P, N // 2 * PACK], BF16, "w_woven1")]
        for u in range(2):
            dst = w_woven[u][:].rearrange("p (c i t) -> p c t i", t=PACK, i=4)
            src = w_raw[u][:].rearrange("p t (c i) -> p c t i", i=4)
            if u == 0:
                nc.gpsimd.tensor_scalar(dst, src, 1.0, 0.0, ALU.mult, ALU.add)
            else:
                nc.vector.tensor_copy(dst, src)
        for u in (1, 0):
            cols = slice(u * N // 2, (u + 1) * N // 2)
            nc.vector.quantize_mx(out=w_words[:, cols].bitcast(FP8X4), scales=w_scales[:, cols], in_=w_woven[u][:])

        out_rows = out.rearrange("(u p) j -> p u j", p=P)
        chunks = S // CHUNK

        def compare(c):
            part = slice(c * CHUNK // 16, (c + 1) * CHUNK // 16)
            second = tile([P, PACK, CHUNK], F32, "second%d" % c)
            diff = tile([P, PACK, CHUNK], F32, "diff%d" % c)
            for t in range(PACK):
                nc.scalar.activation(second[:, t, :], s[t][:].indirect(n2_sb[:, part]), ACT.Copy)
                nc.vector.tensor_tensor(diff[:, t, :], s[t][:].indirect(n1_sb[:, part]), second[:, t, :], ALU.subtract)
            sg = tile([P, PACK, CHUNK], F32, "sg%d" % c)
            if c == chunks - 1:
                for t in range(PACK):
                    nc.scalar.activation(sg[:, t, :], diff[:, t, :], ACT.Sigmoid)
            else:
                nc.scalar.activation(sg[:], diff[:], ACT.Sigmoid)
            return sg

        def finish(c, sg, banks, readers):
            name = "%d" % c
            width = CHUNK
            cols = slice(c * CHUNK, (c + 1) * CHUNK)
            z = tile([P, PACK, CHUNK], BF16, "z" + name)
            for t in range(PACK):
                nc.vector.scalar_tensor_tensor(z[:, t, :], s[t][:, cols], gn_sb[:, t : t + 1], sg[:, t, :], ALU.mult, ALU.mult)
            z_woven = tile([P, width * PACK], BF16, "z_woven" + name)
            (nc.scalar.copy if c in (1, 2) else nc.vector.tensor_copy)(
                z_woven[:].rearrange("p (c i t) -> p c t i", t=PACK, i=4),
                z[:].rearrange("p t (c i) -> p c t i", i=4),
            )
            z_words = tile([P, width], U32, "z_words" + name)
            z_scales = tile([P, width], U8, "z_scales" + name)
            nc.vector.quantize_mx(out=z_words[:].bitcast(FP8X4), scales=z_scales[:], in_=z_woven[:])
            blocks = N // P // len(banks)
            for part, tag in enumerate(banks):
                bank = ps.tile([P, blocks, width], F32, name="out_bank%s_%d" % (name, part), tag=tag)
                for e in range(blocks):
                    u = part * blocks + e
                    nc.tensor.matmul_mx(
                        out=bank[:, e, :],
                        lhsT=w_words[:, u * P : (u + 1) * P].bitcast(FP8X4),
                        lhsT_scale=w_scales[:, u * P : (u + 1) * P],
                        rhs=z_words[:].bitcast(FP8X4),
                        rhs_scale=z_scales[:],
                        start=True,
                        stop=True,
                    )
                result = tile([P, blocks, width], F32, "result%s_%d" % (name, part))
                rows = out_rows[:, part * blocks : (part + 1) * blocks, cols]
                if readers[part] == "vector":
                    nc.vector.tensor_copy(result[:], bank[:])
                else:
                    nc.scalar.copy(result[:], bank[:])
                (nc.scalar if readers[part] == "scalar_own" else nc.sync).dma_start(rows, result[:])

        gates = [compare(0)]
        for c in range(1, chunks):
            gates.append(compare(c))
            finish(c - 1, gates[c - 1], ("bank%d" % (c - 1),), ("scalar",))
        finish(chunks - 1, gates[chunks - 1], ("bank3", "bank4"), ("scalar_own", "vector"))
